import numpy as np, ml_dtypes
CORES = [48,51,52,55]
N = 4
BF = ml_dtypes.bfloat16
def gentries(a):
    return np.ascontiguousarray(a.reshape(8, 16, -1).transpose(0, 2, 1)).reshape(8, -1)
def gtable(e):
    e = np.asarray(e); return np.ascontiguousarray(e.reshape(8, -1, 16).transpose(0, 2, 1)).reshape(128, -1).astype(np.int32)
ND, D, V, Q, TOP = 2048, 8, 192, 512, 1000000
def free(rng):
    s = rng.integers(-TOP, TOP + 1, (8, N * ND, 16))
    c = np.stack([rng.integers(0, (e + 1) * ND, (8, ND, 2)) for e in range(N)], 1).reshape(8, N * ND, 2)
    return s, c
def ledgers(rng):
    s, c = free(rng); G = np.arange(8); roots = []
    ids = np.stack([e * ND + np.argsort(rng.random((8, ND)), 1) for e in range(N)])
    a = rng.integers(-1000, 1001, (8, 1 << D, 16))
    for l in range(D):
        h = 1 << l; n = ids[0][:, h - 1:2 * h - 1]
        s[G[:, None], n] = np.add.reduce(a.reshape(8, h, 2, 1 << (D - 1 - l), 16)[:, :, 0], axis=2)
        if l < D - 1: c[G[:, None], n] = ids[0][:, 2 * h - 1:4 * h - 1].reshape(8, h, 2)
    cur = ids[0][:, 0]
    for e in range(N):
        k = (1 << D) - 1 if e == 0 else 0
        for i in range(V):
            t = rng.integers(0, 1 << D, 8); p = rng.integers(-300, 301, (8, 16)); old = cur; cur = ids[e][:, k]
            for l in range(D):
                b = (t >> (D - 1 - l)) & 1; n = ids[e][:, k]; k += 1
                s[G, n] = s[G, old] + (1 - b)[:, None] * p
                c[G, n] = c[G, old]
                if l < D - 1:
                    old = c[G, old, b]; c[G, n, b] = ids[e][:, k]
            roots.append(cur)
    return s, c, np.stack(roots)
def pack(s, c, ver, day):
    return {"sums": np.ascontiguousarray(s.reshape(8, N, ND, 16).transpose(1, 0, 3, 2)).reshape(N, 128, ND).astype(np.float32),
            "child": np.ascontiguousarray(c.reshape(8, N, 2 * ND).transpose(1, 0, 2)).astype(np.int32),
            "ver": np.stack([gtable(u) for u in ver]), "day": np.stack([gtable(u) for u in day])}
def setup_inputs(rng):
    s, c, roots = ledgers(rng)
    ver = roots[rng.integers(0, N * V, (N, 8, Q)), np.arange(8)[None, :, None]]
    return pack(s, c, ver, rng.integers(0, 1 << D, (N, 8, Q)))
def setup_inputs_any(rng):
    s, c = free(rng)
    return pack(s, c, rng.integers(0, N * ND, (N, 8, Q)), rng.integers(0, 1 << D, (N, 8, Q)))
def setup_inputs_ends(rng):
    s, c = free(rng); e = np.array([0, 1, ND - 2, ND - 1])
    s[:, :, :4] = TOP; s[:, :, 4:8] = -TOP
    c = np.stack([rng.integers(0, q + 1, (8, ND, 2)) * ND + rng.choice(e, (8, ND, 2)) for q in range(N)], 1).reshape(8, N * ND, 2)
    ver = rng.integers(0, N, (N, 8, Q)) * ND + rng.choice(e, (N, 8, Q))
    day = rng.choice(np.array([0, 0, (1 << D) - 1, (1 << D) - 1, (1 << D) - 2] + [1 << l for l in range(D)]), (N, 8, Q))
    ver[:, :, 0] = 0; ver[:, :, Q - 1] = N * ND - 1; day[:, :, 0] = 0; day[:, :, Q - 1] = (1 << D) - 1; day[:, :, 1] = 1; day[:, :, 2] = 1 << (D - 1)
    return pack(s, c, ver, day)
def setup_inputs_crowd(rng):
    s, c = free(rng); q = rng.integers(0, N); p = (q + rng.integers(1, N)) % N
    c[:, q * ND:(q + 1) * ND] = rng.integers(q * ND, (q + 1) * ND, (8, ND, 2))
    ver = rng.integers(q * ND, (q + 1) * ND, (N, 8, Q)); day = rng.integers(0, 1 << D, (N, 8, Q))
    ver[p] = ver[p][:, :1].copy(); day[p] = day[p][:, :1].copy() | 1
    day[p, 0] = (1 << D) - 1; day[p, 7] = (1 << D) - 1
    return pack(s, c, ver, day)
def setup_inputs_older(rng):
    s, c = free(rng)
    for e in range(1, N): c[:, e * ND:(e + 1) * ND] = rng.integers((e - 1) * ND, e * ND, (8, ND, 2))
    c[:, :ND] = np.where(rng.random((8, ND, 2)) < 0.5, np.arange(ND)[None, :, None], c[:, :ND])
    return pack(s, c, rng.integers((N - 1) * ND, N * ND, (N, 8, Q)), rng.integers(0, 1 << D, (N, 8, Q)))
def setup_inputs_spread(rng):
    d = setup_inputs(rng)
    v = rng.integers(-TOP, TOP + 1, (N, 128, ND)) >> (rng.integers(0, 17, (N, 1, ND)) + rng.integers(0, 4, (N, 128, 1)))
    d["sums"] = (v * (rng.random((N, 1, ND)) > 0.0625)).astype(np.float32); return d
def check_inputs(d):
    bad = []; s, c, v, t = d["sums"], d["child"], d["ver"], d["day"]
    if not (np.isfinite(s).all() and (np.abs(s) <= TOP).all() and (s == np.floor(s)).all()): bad.append("sums")
    if not ((c >= 0) & (c < ((np.arange(N) + 1) * ND)[:, None, None])).all(): bad.append("child")
    if not ((v >= 0) & (v < N * ND)).all(): bad.append("ver")
    if not ((t >= 0) & (t < (1 << D))).all(): bad.append("day")
    return bad
def reference(sums, child, ver, day):
    s = np.ascontiguousarray(sums.reshape(N, 8, 16, ND).transpose(1, 0, 3, 2)).reshape(8, N * ND, 16).astype(np.float64)
    c = np.ascontiguousarray(child.transpose(1, 0, 2)).reshape(8, 2 * N * ND).astype(np.int64)
    g = np.arange(8)[:, None]; y = np.zeros((N, 8, Q, 16), np.float64)
    for r in range(N):
        n = gentries(ver[r]).astype(np.int64); t = gentries(day[r]).astype(np.int64)
        for l in range(D - 1, -1, -1):
            b = (t >> l) & 1
            y[r] += b[:, :, None] * s[g, n]
            n = c[g, 2 * n + b]
    return {"y": np.ascontiguousarray(y.transpose(0, 1, 3, 2)).reshape(N, 128, Q).astype(np.float32)}

@@ -1,0 +1,300 @@
+from concourse.bass import DstId, RemoteDMATransfer
+from concourse.mybir import AluOpType, ActivationFunctionType
+
+N, ND, D, Q = 4, 2048, 8, 512
+K = Q // 16
+KV = 16
+KG = 16
+QV, QS = 16 * KV, Q - 16 * KV
+CHUNKS = [(0, 512), (512, 1024), (1024, 1536), (1536, 2048)]
+EARLY = {}
+W = 2 * ND
+
+SCRATCH = {
+    "ci": ("sbuf", [128, 256], "int32"),
+    "hi": ("sbuf", [128, 256], "bfloat16"),
+    "lo": ("sbuf", [128, 256], "bfloat16"),
+    "td": ("dram", [2 * N, 128, 256], "bfloat16"),
+    "tw": ("sbuf", [128, N * W], "bfloat16"),
+    "sw": ("sbuf", [128, N * ND + 8], "float32"),
+    "vi": ("sbuf", [128, K], "int32"),
+    "di": ("sbuf", [128, K], "int32"),
+    "bi": ("sbuf", [128, D * K], "int32"),
+    "badd": ("sbuf", [128, D * K], "bfloat16"),
+    "cmax": ("sbuf", [128, D * K], "float32"),
+    "v2": ("sbuf", [128, K], "float32"),
+    "i0f": ("sbuf", [128, K], "float32"),
+    "idx": ("sbuf", [128, D * K], "uint16"),
+    "off": ("sbuf", [128, D * K], "uint16"),
+    "u": ("sbuf", [128, D * K], "float32"),
+    "G": ("sbuf", [128, (D - 1) * Q], "bfloat16"),
+    "val": ("sbuf", [128, 144], "float32"),
+    "pi": ("sbuf", [128, 8], "int32"),
+    "pa": ("sbuf", [128, 8], "int32"),
+    "pf": ("sbuf", [128, 8], "float32"),
+    "B": ("sbuf", [128, 144], "bfloat16"),
+    "Ib": ("sbuf", [128, 128], "bfloat16"),
+    "If": ("sbuf", [128, 128], "float32"),
+    "acc": ("sbuf", [128, QV], "float32"),
+    "gs": ("sbuf", [128, D * QS], "float32"),
+    "out2": ("sbuf", [128, QS], "float32"),
+    "pacc": ("psum", [128, 512], "float32"),
+}
+for _t in range(D - 1):
+    SCRATCH["ps%d" % _t] = ("psum", [128, 512], "float32")
+
+SEMAPHORES = (["tab%d" % r for r in range(N)] + ["h%d" % c for c in range(len(CHUNKS))]
+              + ["sarr", "tleft", "sleft"] + ["s%d" % i for i in range(130)])
+
+A = AluOpType
+COPY = ActivationFunctionType.Copy
+
+
+def bits(engs):
+    m = 0
+    for e in engs:
+        m |= 1 << e
+    return m
+
+
+def dst_id(topo, c):
+    rid, pid, _ = topo.addr(c)
+    return DstId(rid=rid, pnc=pid)
+
+
+def roles(T, topo):
+    cores = list(T.cores)
+    free = [c for c in topo.cores_of(cores[0]) if c not in cores]
+    out = []
+    for r, c in enumerate(cores):
+        near = [q for q in range(N) if topo.die(cores[q]) == topo.die(c)]
+        far = [q for q in range(N) if q not in near]
+        helpers = [h for h in free if topo.die(h) != topo.die(c)]
+        i = near.index(r)
+        out.append(([q for q in near if q != r][0], far[i:] + far[:i], helpers[i]))
+    return out
+
+
+def helper_program(g, core, T, topo, e, far):
+    cores = list(T.cores)
+    S = T.sem
+    engs = topo.engines(core, cores[far[0]])
+    half = len(engs) // 2
+    for c, (a, b) in enumerate(CHUNKS):
+        g.wait_ge(S["h%d" % c], half)
+        ap = T.sw[:, e * ND + a:e * ND + b]
+        g.remote_dma_fused([
+            RemoteDMATransfer(dst_ids=[dst_id(topo, cores[q])], dma_engine_mask=bits(engs[i::2]),
+                              remote_sem=S.sarr, src=ap, dst=ap) for i, q in enumerate(far)], local_sem=S.sleft)
+    g.wait_ge(S.sleft, 2 * half * len(CHUNKS))
+
+
+def rank_program(g, core, T, topo):
+    rank = T.rank_of(core)
+    cores = list(T.cores)
+    rl = roles(T, topo)
+    if rank is None:
+        for e in range(N):
+            if rl[e][2] == core:
+                helper_program(g, core, T, topo, e, rl[e][1])
+        return
+    S = T.sem
+    V, SC, PE, SY = g.vector, g.scalar, g.tensor, g.sync
+    partner, far, helper = rl[rank]
+    engs = topo.engines(core, cores[partner])
+    half = len(engs) // 2
+    nsem = [0]
+
+    def new():
+        nsem[0] += 1
+        return S["s%d" % (nsem[0] - 1)]
+
+    def sig(ins, n=1):
+        s = new()
+        ins.then_inc(s, n)
+        return (s, n)
+
+    def group(inss, n=1):
+        s = new()
+        for i in inss:
+            i.then_inc(s, n)
+        return (s, n * len(inss))
+
+    def wait(q, *evs):
+        for s, n in evs:
+            q.wait_ge(s, n)
+
+    tw, sw = T.tw, T.sw
+    c_own, c_par, c_f0, c_f1 = rank * W, partner * W, far[0] * W, far[1] * W
+
+    e_ci = sig(SY.dma_start(T.ci[:], T.child[:]), 16)
+    e_ld = [sig(SY.dma_start(sw[:, rank * ND + a:rank * ND + b], T.sums[:, a:b]), 16) for a, b in CHUNKS]
+    e_q = group([SY.dma_start(T.di[:], T.day[:]), SY.dma_start(T.vi[:], T.ver[:])], 16)
+
+    e_val = group([g.iota(T.val[:], [[1, 144]], 0, -1, allow_small_or_imprecise_dtypes=True),
+                   g.iota(T.pi[:, 0:1], [[1, 1]], 127, -1)])
+    e_fg = sig(g.iota(tw[:, c_f0 + 2368:c_f0 + 3008], [[0, 640]], 0, 0, allow_small_or_imprecise_dtypes=True))
+
+    e_fz = sig(V.memset(tw[:, c_f0:c_f0 + 1024], 0.0))
+    s_own = new()
+    V.memset(tw[:, c_own:c_own + 2560], 0.0).then_inc(s_own, 1)
+    wait(V, e_ci)
+    e_hi = sig(V.tensor_copy(T.hi[:], T.ci[:]))
+    wait(V, e_hi)
+    e_lo = sig(V.tensor_tensor(T.lo[:], T.ci[:], T.hi[:], A.subtract))
+    V.memset(tw[:, c_own + 2560:c_own + W], 0.0).then_inc(s_own, 1)
+    e_own = (s_own, 2)
+    e_fpar = sig(V.memset(tw[:, c_par:c_par + W], 0.0))
+    e_ff0 = sig(V.memset(tw[:, c_f0 + 3008:c_f0 + W], 0.0))
+
+    wait(SC, e_fz)
+    z = tw[:, c_f0:c_f0 + 1024]
+    e_ff1 = group([SC.activation(tw[:, c_f1 + a:c_f1 + a + 1024], z, COPY) for a in range(0, W, 1024)])
+    e_fs = group([SC.activation(tw[:, c_f0 + 1024:c_f0 + 2048], z, COPY),
+                  SC.activation(tw[:, c_f0 + 2048:c_f0 + 2368], tw[:, c_f0:c_f0 + 320], COPY)])
+    filled = {partner: [e_fpar], far[1]: [e_ff1], far[0]: [e_ff1, e_fs, e_fg, e_ff0]}
+
+    others = [partner] + far
+    wait(g, e_lo)
+    g.remote_dma_fused([
+        RemoteDMATransfer(dst_ids=[dst_id(topo, cores[q]) for q in others], dma_engine_mask=bits(engs[i::2]),
+                          remote_sem=S["tab%d" % rank], srcs=[src[:]], dsts=[T.td[2 * rank + i] for q in others])
+        for i, src in enumerate((T.hi, T.lo))], local_sem=S.tleft)
+
+    tdma = new()
+    ntd = 0
+    wait(SY, e_lo, e_own)
+    for i, src in enumerate((T.hi, T.lo)):
+        SY.dma_start(tw[i::16, c_own:c_own + W], src[:]).then_inc(tdma, 16)
+        ntd += 16
+    for r in (far[1], partner, far[0]):
+        qs = (SY, SC) if r == far[0] else (SY, SY)
+        for i, q in enumerate(qs):
+            if i == 0 or q is not qs[0]:
+                wait(q, *filled[r])
+                q.wait_ge(S["tab%d" % r], 2 * half)
+            q.dma_start(tw[i::16, r * W:(r + 1) * W], T.td[2 * r + i]).then_inc(tdma, 16)
+            ntd += 16
+    e_tw = (tdma, ntd)
+    s_iss = new()
+    SY.sem_inc(s_iss, 1)
+
+    for c, (a, b) in enumerate(CHUNKS):
+        if c == 1:
+            g.wait_ge(s_iss, 1)
+        wait(g, e_ld[c])
+        ap = sw[:, rank * ND + a:rank * ND + b]
+        g.remote_dma_fused([
+            RemoteDMATransfer(dst_ids=[dst_id(topo, helper)], dma_engine_mask=bits(engs[0::2]),
+                              remote_sem=S["h%d" % c], src=ap, dst=ap),
+            RemoteDMATransfer(dst_ids=[dst_id(topo, cores[partner])], dma_engine_mask=bits(engs[1::2]),
+                              remote_sem=S.sarr, src=ap, dst=ap)], local_sem=S.sleft)
+    g.wait_ge(S.tleft, 2 * half)
+    g.wait_ge(S.sleft, 2 * half * len(CHUNKS))
+    e_sums = [(S.sarr, 3 * half * len(CHUNKS))] + e_ld
+
+    def col(t, a=0, b=K):
+        return slice(t * K + a, t * K + b)
+
+    wait(V, e_q, e_val)
+    e_bi = group([V.tensor_scalar(T.bi[:, col(t)], T.di[:], D - 1 - t, 1, A.logical_shift_right, A.bitwise_and)
+                  for t in range(D)]
+                 + [V.tensor_scalar(T.v2[:], T.vi[:], 2.0, None, A.mult),
+                    V.tensor_scalar(T.pa[:, 0:1], T.pi[:, 0:1], 15, None, A.bitwise_and)])
+    wait(V, e_bi)
+    e_c1 = group([V.tensor_tensor(T.i0f[:], T.v2[:], T.bi[:, col(0)], A.add),
+                  V.tensor_copy(T.pf[:, 0:1], T.pa[:, 0:1]),
+                  V.tensor_copy(T.badd[:, K:(D - 1) * K], T.bi[:, K:(D - 1) * K]),
+                  V.tensor_scalar(T.badd[:, col(D - 1)], T.bi[:, col(D - 1)], -16384.0, 16384.0, A.mult, A.add),
+                  V.tensor_scalar(T.Ib[:], T.val[:, 0:128], 0.0, None, A.is_equal)])
+    wait(V, e_c1)
+    e_c2 = group([V.tensor_copy(T.idx[:, col(0)], T.i0f[:]),
+                  V.tensor_scalar(T.B[:], T.val[:], T.pf[:, 0:1], 2.0, A.is_equal, A.mult),
+                  V.tensor_scalar(T.cmax[:, 0:(D - 1) * K], T.bi[:, 0:(D - 1) * K], -16385.0, 16385.0, A.mult, A.add),
+                  V.tensor_scalar(T.If[:], T.val[:, 0:128], 0.0, None, A.is_equal),
+                  V.memset(sw[:, N * ND:N * ND + 8], 0.0)])
+    wait(V, e_c2)
+    wait(PE, e_c2)
+    wait(SC, e_c2)
+
+    e_off = {}
+
+    def offsets(t, src):
+        e_u = sig(V.tensor_tensor(T.u[:, col(t)], src, T.cmax[:, col(t)], A.max))
+        wait(V, e_u)
+        e_off[t] = sig(V.tensor_scalar(T.off[:, col(t)], T.u[:, col(t)], -1.0, 0.5, A.add, A.mult))
+
+    st = {"v": None, "first": True, "n": 0}
+    pend = []
+
+    def totals_v(t):
+        if st["v"] is None:
+            wait(V, *e_sums)
+        else:
+            wait(V, st["v"])
+        wait(V, e_off[t])
+        src = sw[:].indirect(T.off[:, col(t, 0, KV)])
+        if st["v"] is None:
+            st["v"] = sig(V.tensor_copy(T.acc[:], src))
+        else:
+            st["v"] = sig(V.tensor_tensor(T.acc[:], src, T.acc[:], A.add))
+
+    def totals_s(t):
+        if st["first"]:
+            wait(SC, *e_sums)
+            st["first"] = False
+        wait(SC, e_off[t])
+        pend.append((t, sig(SC.activation(T.gs[:, t * QS:(t + 1) * QS], sw[:].indirect(T.off[:, col(t, KV, K)]),
+                                          COPY))))
+
+    def totals_pe():
+        last = None
+        while pend:
+            t, ev = pend.pop(0)
+            wait(PE, ev)
+            last = PE.matmul(T.pacc[:, 0:QS], T.If[:], T.gs[:, t * QS:(t + 1) * QS], st["n"] == 0, st["n"] == D - 1)
+            st["n"] += 1
+        return last
+
+    wait(V, e_tw)
+    wait(SC, e_tw)
+    done = []
+    e_pe = None
+    for t in range(D - 1):
+        ps = T["ps%d" % t]
+        if t > 0:
+            wait(V, e_pe)
+            e_idx = sig(V.tensor_copy(T.idx[:, col(t)], T["ps%d" % (t - 1)][:, 0:K]))
+            wait(V, e_idx)
+            wait(SC, e_idx)
+        g0 = t * Q
+        e_g = group([V.tensor_copy(T.G[:, g0:g0 + 16 * KG], tw[:].indirect(T.idx[:, col(t, 0, KG)])),
+                     SC.activation(T.G[:, g0 + 16 * KG:g0 + Q], tw[:].indirect(T.idx[:, col(t, KG, K)]), COPY)])
+        PE.matmul(ps[:, 0:K], T.Ib[:], T.badd[:, col(t + 1)], True, False)
+        totals_pe()
+        wait(PE, e_g)
+        for s in range(16):
+            mm = PE.matmul(ps[:, 0:K], T.B[:, 15 - s:143 - s], T.G[:, g0 + s:g0 + Q:16], False, s == 15)
+        e_pe = sig(mm)
+        offsets(t, T["ps%d" % (t - 1)][:, 0:K] if t > 0 else T.i0f[:])
+        for x in EARLY.get(t, []):
+            totals_v(x)
+            totals_s(x)
+            done.append(x)
+
+    rest = [t for t in range(D - 1) if t not in done]
+    totals_v(rest[0])
+    wait(V, e_pe)
+    e_off[D - 1] = sig(V.tensor_scalar(T.off[:, col(D - 1)], T["ps%d" % (D - 2)][:, 0:K], 0.5, float(N * ND),
+                                       A.mult, A.min))
+    for t in rest[1:] + [D - 1]:
+        totals_v(t)
+    for t in rest + [D - 1]:
+        totals_s(t)
+    e_acc = sig(totals_pe())
+
+    wait(SY, st["v"])
+    wait(SY, sig(SY.dma_start(T.y[:, 0:QV], T.acc[:]), 16))
+    wait(SC, e_acc)
+    wait(SC, sig(SC.activation(T.out2[:], T.pacc[:, 0:QS], COPY)))
+    wait(SC, sig(SC.dma_start(T.y[:, QV:Q], T.out2[:]), 16))

@@ -6,8 +6,14 @@ K = Q // 16
 KV = 16
 KG = 16
 QV, QS = 16 * KV, Q - 16 * KV
+VPARTS = [(0, KV // 4 * 2), (KV // 4 * 2, KV)]
 CHUNKS = [(0, 512), (512, 1024), (1024, 1536), (1536, 2048)]
-EARLY = {}
+FRONT = 3
+CALLS = [(("h", 0), ("h", 1)), (("h", 2), ("p", 0)), (("h", 3), ("p", 1)), (("p", 2), ("p", 3))]
+GAP = 1
+EARLY_V = {5: [0]}
+EARLY_S = {5: [0, 1]}
+PE_EARLY = True
 W = 2 * ND
 
 SCRATCH = {
@@ -44,7 +50,7 @@ for _t in range(D - 1):
     SCRATCH["ps%d" % _t] = ("psum", [128, 512], "float32")
 
 SEMAPHORES = (["tab%d" % r for r in range(N)] + ["h%d" % c for c in range(len(CHUNKS))]
-              + ["sarr", "tleft", "sleft"] + ["s%d" % i for i in range(130)])
+              + ["sarr", "tleft", "sleft", "zarr", "zleft"] + ["s%d" % i for i in range(130)])
 
 A = AluOpType
 COPY = ActivationFunctionType.Copy
@@ -127,13 +133,13 @@ def rank_program(g, core, T, topo):
     tw, sw = T.tw, T.sw
     c_own, c_par, c_f0, c_f1 = rank * W, partner * W, far[0] * W, far[1] * W
 
-    e_ci = sig(SY.dma_start(T.ci[:], T.child[:]), 16)
-    e_ld = [sig(SY.dma_start(sw[:, rank * ND + a:rank * ND + b], T.sums[:, a:b]), 16) for a, b in CHUNKS]
-    e_q = group([SY.dma_start(T.di[:], T.day[:]), SY.dma_start(T.vi[:], T.ver[:])], 16)
+    def load(c):
+        a, b = CHUNKS[c]
+        return sig(SY.dma_start(sw[:, rank * ND + a:rank * ND + b], T.sums[:, a:b]), 16)
 
-    e_val = group([g.iota(T.val[:], [[1, 144]], 0, -1, allow_small_or_imprecise_dtypes=True),
-                   g.iota(T.pi[:, 0:1], [[1, 1]], 127, -1)])
-    e_fg = sig(g.iota(tw[:, c_f0 + 2368:c_f0 + 3008], [[0, 640]], 0, 0, allow_small_or_imprecise_dtypes=True))
+    e_ci = sig(SY.dma_start(T.ci[:], T.child[:]), 16)
+    e_ld = [load(c) for c in range(FRONT)]
+    e_q = group([SY.dma_start(T.di[:], T.day[:]), SY.dma_start(T.vi[:], T.ver[:])], 16)
 
     e_fz = sig(V.memset(tw[:, c_f0:c_f0 + 1024], 0.0))
     s_own = new()
@@ -145,15 +151,22 @@ def rank_program(g, core, T, topo):
     V.memset(tw[:, c_own + 2560:c_own + W], 0.0).then_inc(s_own, 1)
     e_own = (s_own, 2)
     e_fpar = sig(V.memset(tw[:, c_par:c_par + W], 0.0))
-    e_ff0 = sig(V.memset(tw[:, c_f0 + 3008:c_f0 + W], 0.0))
+    e_ff0 = sig(V.memset(tw[:, c_f0 + 3248:c_f0 + W], 0.0))
 
     wait(SC, e_fz)
     z = tw[:, c_f0:c_f0 + 1024]
     e_ff1 = group([SC.activation(tw[:, c_f1 + a:c_f1 + a + 1024], z, COPY) for a in range(0, W, 1024)])
-    e_fs = group([SC.activation(tw[:, c_f0 + 1024:c_f0 + 2048], z, COPY),
-                  SC.activation(tw[:, c_f0 + 2048:c_f0 + 2368], tw[:, c_f0:c_f0 + 320], COPY)])
-    filled = {partner: [e_fpar], far[1]: [e_ff1], far[0]: [e_ff1, e_fs, e_fg, e_ff0]}
+    e_fs = group([SC.activation(tw[:, c_f0 + 2048:c_f0 + 3072], z, COPY),
+                  SC.activation(tw[:, c_f0 + 3072:c_f0 + 3248], tw[:, c_f0:c_f0 + 176], COPY)])
+    filled = {partner: [e_fpar], far[1]: [e_ff1],
+              far[0]: [e_ff1, e_fs, e_ff0, (S.zarr, 2 * half), (S.zleft, 2 * half)]}
 
+    i_val = g.iota(T.val[:], [[1, 144]], 0, -1, allow_small_or_imprecise_dtypes=True)
+    wait(g, e_fz)
+    c_z = rl[partner][1][0] * W
+    rid, pid, _ = topo.addr(cores[partner])
+    g.remote_dma(tw[:, c_z + 1024:c_z + 2048], z, S.zarr, S.zleft, pid, rid, bits(engs))
+    e_val = group([i_val, g.iota(T.pi[:, 0:1], [[1, 1]], 127, -1)])
     others = [partner] + far
     wait(g, e_lo)
     g.remote_dma_fused([
@@ -178,66 +191,78 @@ def rank_program(g, core, T, topo):
     e_tw = (tdma, ntd)
     s_iss = new()
     SY.sem_inc(s_iss, 1)
+    e_ld += [load(c) for c in range(FRONT, len(CHUNKS))]
 
-    for c, (a, b) in enumerate(CHUNKS):
-        if c == 1:
+    seen = []
+    for n, call in enumerate(CALLS):
+        if n == GAP:
             g.wait_ge(s_iss, 1)
-        wait(g, e_ld[c])
-        ap = sw[:, rank * ND + a:rank * ND + b]
-        g.remote_dma_fused([
-            RemoteDMATransfer(dst_ids=[dst_id(topo, helper)], dma_engine_mask=bits(engs[0::2]),
-                              remote_sem=S["h%d" % c], src=ap, dst=ap),
-            RemoteDMATransfer(dst_ids=[dst_id(topo, cores[partner])], dma_engine_mask=bits(engs[1::2]),
-                              remote_sem=S.sarr, src=ap, dst=ap)], local_sem=S.sleft)
+        trs = []
+        for i, (to, c) in enumerate(call):
+            if c not in seen:
+                wait(g, e_ld[c])
+                seen.append(c)
+            ap = sw[:, rank * ND + CHUNKS[c][0]:rank * ND + CHUNKS[c][1]]
+            trs.append(RemoteDMATransfer(
+                dst_ids=[dst_id(topo, helper if to == "h" else cores[partner])], dma_engine_mask=bits(engs[i::2]),
+                remote_sem=S["h%d" % c] if to == "h" else S.sarr, src=ap, dst=ap))
+        g.remote_dma_fused(trs, local_sem=S.sleft)
     g.wait_ge(S.tleft, 2 * half)
-    g.wait_ge(S.sleft, 2 * half * len(CHUNKS))
+    g.wait_ge(S.sleft, 2 * half * len(CALLS))
     e_sums = [(S.sarr, 3 * half * len(CHUNKS))] + e_ld
 
     def col(t, a=0, b=K):
         return slice(t * K + a, t * K + b)
 
+    last = D - 1
     wait(V, e_q, e_val)
-    e_bi = group([V.tensor_scalar(T.bi[:, col(t)], T.di[:], D - 1 - t, 1, A.logical_shift_right, A.bitwise_and)
-                  for t in range(D)]
-                 + [V.tensor_scalar(T.v2[:], T.vi[:], 2.0, None, A.mult),
-                    V.tensor_scalar(T.pa[:, 0:1], T.pi[:, 0:1], 15, None, A.bitwise_and)])
+    e_bi = group([V.tensor_scalar(T.pa[:, 0:1], T.pi[:, 0:1], 15, None, A.bitwise_and),
+                  V.tensor_scalar(T.v2[:], T.vi[:], 2.0, None, A.mult),
+                  V.tensor_scalar(T.bi[:, col(0)], T.di[:], last, 1, A.logical_shift_right, A.bitwise_and)])
+    e_b2 = group([V.tensor_scalar(T.bi[:, col(t)], T.di[:], last - t, 1, A.logical_shift_right, A.bitwise_and)
+                  for t in range(1, D)])
     wait(V, e_bi)
-    e_c1 = group([V.tensor_tensor(T.i0f[:], T.v2[:], T.bi[:, col(0)], A.add),
-                  V.tensor_copy(T.pf[:, 0:1], T.pa[:, 0:1]),
-                  V.tensor_copy(T.badd[:, K:(D - 1) * K], T.bi[:, K:(D - 1) * K]),
-                  V.tensor_scalar(T.badd[:, col(D - 1)], T.bi[:, col(D - 1)], -16384.0, 16384.0, A.mult, A.add),
-                  V.tensor_scalar(T.Ib[:], T.val[:, 0:128], 0.0, None, A.is_equal)])
+    e_c1 = group([V.tensor_copy(T.pf[:, 0:1], T.pa[:, 0:1]),
+                  V.tensor_tensor(T.i0f[:], T.v2[:], T.bi[:, col(0)], A.add)])
+    wait(V, e_b2)
+    c2 = [V.tensor_copy(T.badd[:, K:last * K], T.bi[:, K:last * K]),
+          V.tensor_scalar(T.Ib[:], T.val[:, 0:128], 0.0, None, A.is_equal)]
     wait(V, e_c1)
-    e_c2 = group([V.tensor_copy(T.idx[:, col(0)], T.i0f[:]),
-                  V.tensor_scalar(T.B[:], T.val[:], T.pf[:, 0:1], 2.0, A.is_equal, A.mult),
-                  V.tensor_scalar(T.cmax[:, 0:(D - 1) * K], T.bi[:, 0:(D - 1) * K], -16385.0, 16385.0, A.mult, A.add),
-                  V.tensor_scalar(T.If[:], T.val[:, 0:128], 0.0, None, A.is_equal),
+    e_i0 = sig(V.tensor_copy(T.idx[:, col(0)], T.i0f[:]))
+    c2 += [V.tensor_scalar(T.B[:], T.val[:], T.pf[:, 0:1], 2.0, A.is_equal, A.mult),
+           V.tensor_scalar(T.badd[:, col(last)], T.bi[:, col(last)], -16384.0, 16384.0, A.mult, A.add),
+           V.tensor_scalar(T.If[:], T.val[:, 0:128], 0.0, None, A.is_equal)]
+    wait(PE, group(c2))
+    e_c3 = group([V.tensor_scalar(T.cmax[:, 0:last * K], T.bi[:, 0:last * K], -16385.0, 16385.0, A.mult, A.add),
                   V.memset(sw[:, N * ND:N * ND + 8], 0.0)])
-    wait(V, e_c2)
-    wait(PE, e_c2)
-    wait(SC, e_c2)
 
-    e_off = {}
+    e_u, e_off = {}, {}
 
-    def offsets(t, src):
-        e_u = sig(V.tensor_tensor(T.u[:, col(t)], src, T.cmax[:, col(t)], A.max))
-        wait(V, e_u)
+    def off_a(t, src):
+        e_u[t] = sig(V.tensor_tensor(T.u[:, col(t)], src, T.cmax[:, col(t)], A.max))
+
+    def off_b(t):
+        wait(V, e_u[t])
         e_off[t] = sig(V.tensor_scalar(T.off[:, col(t)], T.u[:, col(t)], -1.0, 0.5, A.add, A.mult))
 
     st = {"v": None, "first": True, "n": 0}
     pend = []
 
     def totals_v(t):
-        if st["v"] is None:
+        first = st["v"] is None
+        if first:
             wait(V, *e_sums)
-        else:
-            wait(V, st["v"])
         wait(V, e_off[t])
-        src = sw[:].indirect(T.off[:, col(t, 0, KV)])
-        if st["v"] is None:
-            st["v"] = sig(V.tensor_copy(T.acc[:], src))
-        else:
-            st["v"] = sig(V.tensor_tensor(T.acc[:], src, T.acc[:], A.add))
+        evs = []
+        for i, (a, b) in enumerate(VPARTS):
+            src = sw[:].indirect(T.off[:, col(t, a, b)])
+            acc = T.acc[:, 16 * a:16 * b]
+            if first:
+                evs.append(sig(V.tensor_copy(acc, src)))
+            else:
+                wait(V, st["v"][i])
+                evs.append(sig(V.tensor_tensor(acc, src, acc, A.add)))
+        st["v"] = evs
 
     def totals_s(t):
         if st["first"]:
@@ -248,52 +273,64 @@ def rank_program(g, core, T, topo):
                                           COPY))))
 
     def totals_pe():
-        last = None
+        mm = None
         while pend:
             t, ev = pend.pop(0)
             wait(PE, ev)
-            last = PE.matmul(T.pacc[:, 0:QS], T.If[:], T.gs[:, t * QS:(t + 1) * QS], st["n"] == 0, st["n"] == D - 1)
+            mm = PE.matmul(T.pacc[:, 0:QS], T.If[:], T.gs[:, t * QS:(t + 1) * QS], st["n"] == 0, st["n"] == D - 1)
             st["n"] += 1
-        return last
+        return mm
 
-    wait(V, e_tw)
-    wait(SC, e_tw)
-    done = []
+    wait(V, e_i0, e_c3, e_tw)
+    wait(SC, e_i0, e_tw)
+    done_v, done_s = [], []
     e_pe = None
-    for t in range(D - 1):
+    for t in range(last):
         ps = T["ps%d" % t]
+        res = T.i0f[:]
         if t > 0:
+            res = T["ps%d" % (t - 1)][:, 0:K]
             wait(V, e_pe)
-            e_idx = sig(V.tensor_copy(T.idx[:, col(t)], T["ps%d" % (t - 1)][:, 0:K]))
+            e_idx = sig(V.tensor_copy(T.idx[:, col(t)], res))
+            off_a(t, res)
             wait(V, e_idx)
             wait(SC, e_idx)
         g0 = t * Q
         e_g = group([V.tensor_copy(T.G[:, g0:g0 + 16 * KG], tw[:].indirect(T.idx[:, col(t, 0, KG)])),
                      SC.activation(T.G[:, g0 + 16 * KG:g0 + Q], tw[:].indirect(T.idx[:, col(t, KG, K)]), COPY)])
         PE.matmul(ps[:, 0:K], T.Ib[:], T.badd[:, col(t + 1)], True, False)
-        totals_pe()
+        if PE_EARLY:
+            totals_pe()
         wait(PE, e_g)
         for s in range(16):
             mm = PE.matmul(ps[:, 0:K], T.B[:, 15 - s:143 - s], T.G[:, g0 + s:g0 + Q:16], False, s == 15)
         e_pe = sig(mm)
-        offsets(t, T["ps%d" % (t - 1)][:, 0:K] if t > 0 else T.i0f[:])
-        for x in EARLY.get(t, []):
+        if t == 0:
+            off_a(0, res)
+        else:
+            off_b(t)
+        if t == 1:
+            off_b(0)
+        for x in EARLY_V.get(t, []):
             totals_v(x)
+            done_v.append(x)
+        for x in EARLY_S.get(t, []):
             totals_s(x)
-            done.append(x)
+            done_s.append(x)
 
-    rest = [t for t in range(D - 1) if t not in done]
+    rest = [t for t in range(last) if t not in done_v]
     totals_v(rest[0])
     wait(V, e_pe)
-    e_off[D - 1] = sig(V.tensor_scalar(T.off[:, col(D - 1)], T["ps%d" % (D - 2)][:, 0:K], 0.5, float(N * ND),
-                                       A.mult, A.min))
-    for t in rest[1:] + [D - 1]:
+    e_off[last] = sig(V.tensor_scalar(T.off[:, col(last)], T["ps%d" % (last - 1)][:, 0:K], 0.5, float(N * ND),
+                                      A.mult, A.min))
+    for t in rest[1:] + [last]:
         totals_v(t)
-    for t in rest + [D - 1]:
-        totals_s(t)
+    for t in range(D):
+        if t not in done_s:
+            totals_s(t)
     e_acc = sig(totals_pe())
 
-    wait(SY, st["v"])
+    wait(SY, *st["v"])
     wait(SY, sig(SY.dma_start(T.y[:, 0:QV], T.acc[:]), 16))
     wait(SC, e_acc)
     wait(SC, sig(SC.activation(T.out2[:], T.pacc[:, 0:QS], COPY)))

@@ -3,17 +3,26 @@ from concourse.mybir import AluOpType, ActivationFunctionType
 
 N, ND, D, Q = 4, 2048, 8, 512
 K = Q // 16
+H = K // 2
 KV = 16
-KG = 16
 QV, QS = 16 * KV, Q - 16 * KV
-VPARTS = [(0, KV // 4 * 2), (KV // 4 * 2, KV)]
+VHALVES = [(0, KV // 4 * 2), (KV // 4 * 2, KV)]
+SHALVES = [(KV, KV + 10), (KV + 10, K)]
 CHUNKS = [(0, 512), (512, 1024), (1024, 1536), (1536, 2048)]
-FRONT = 3
-CALLS = [(("h", 0), ("h", 1)), (("h", 2), ("p", 0)), (("h", 3), ("p", 1)), (("p", 2), ("p", 3))]
+CALLS = [(("h", 0, 1),), (("h", 1, 2), ("p", 1, 2)), (("h", 2, 3), ("p", 2, 3)), (("a", 3, 4), ("p", 3, 4)), (("b", 3, 4),)]
+HCALLS = [(("p", 0, 1), ("a", 0, 1)), (("b", 0, 1),), (("a", 1, 2), ("b", 1, 2)), (("a", 2, 3), ("b", 2, 3))]
 GAP = 1
-EARLY_V = {5: [0]}
-EARLY_S = {5: [0, 1]}
-PE_EARLY = True
+LOADS = [[(0, 2)], [(2, 3), (3, 4)]]
+ZB = 256
+LZ = 1792
+V1 = 2048
+SF = 640
+TWO = 5
+PRE = 4
+KG = [8, 8, 8, 8, 8, 8, 8, 8, 8, 8, 16, 16]
+SLOT = ["", "", "", "", "", "", "", "", "", "", "", "a57"]
+JOBS = ["b4 b5 If", "b6 b7 zero", "w", "c0", "c1", "w7", "", "", "", "n m", "H H S S S", "o H H"]
+PJ = [0, 0, 0, 0, 0, 0, 0, 0, 0, 0, 0, 3]
 W = 2 * ND
 
 SCRATCH = {
@@ -32,21 +41,20 @@ SCRATCH = {
     "i0f": ("sbuf", [128, K], "float32"),
     "idx": ("sbuf", [128, D * K], "uint16"),
     "off": ("sbuf", [128, D * K], "uint16"),
+    "nf": ("sbuf", [128, D * K], "float32"),
     "u": ("sbuf", [128, D * K], "float32"),
     "G": ("sbuf", [128, (D - 1) * Q], "bfloat16"),
-    "val": ("sbuf", [128, 144], "float32"),
-    "pi": ("sbuf", [128, 8], "int32"),
-    "pa": ("sbuf", [128, 8], "int32"),
-    "pf": ("sbuf", [128, 8], "float32"),
+    "two": ("sbuf", [128, 8], "bfloat16"),
     "B": ("sbuf", [128, 144], "bfloat16"),
     "Ib": ("sbuf", [128, 128], "bfloat16"),
     "If": ("sbuf", [128, 128], "float32"),
     "acc": ("sbuf", [128, QV], "float32"),
     "gs": ("sbuf", [128, D * QS], "float32"),
     "out2": ("sbuf", [128, QS], "float32"),
-    "pacc": ("psum", [128, 512], "float32"),
+    "pacc0": ("psum", [128, 512], "float32"),
+    "pacc1": ("psum", [128, 512], "float32"),
 }
-for _t in range(D - 1):
+for _t in range(6):
     SCRATCH["ps%d" % _t] = ("psum", [128, 512], "float32")
 
 SEMAPHORES = (["tab%d" % r for r in range(N)] + ["h%d" % c for c in range(len(CHUNKS))]
@@ -54,6 +62,7 @@ SEMAPHORES = (["tab%d" % r for r in range(N)] + ["h%d" % c for c in range(len(CH
 
 A = AluOpType
 COPY = ActivationFunctionType.Copy
+IDENT = ActivationFunctionType.Identity
 
 
 def bits(engs):
@@ -81,18 +90,34 @@ def roles(T, topo):
     return out
 
 
-def helper_program(g, core, T, topo, e, far):
+def piece(T, e, c0, c1):
+    return T.sw[:, e * ND + CHUNKS[c0][0]:e * ND + CHUNKS[c1 - 1][1]]
+
+
+def landing(n_eng):
+    at_helper = {c0: (c1, n_eng // len(call)) for call in CALLS for to, c0, c1 in call if to == "h"}
+    at_rank = sum(n_eng // len(call) for call in CALLS for to, c0, c1 in call if to != "h")
+    return at_helper, at_rank + n_eng * len(HCALLS)
+
+
+def helper_program(g, core, T, topo, e, partner, far):
     cores = list(T.cores)
     S = T.sem
     engs = topo.engines(core, cores[far[0]])
-    half = len(engs) // 2
-    for c, (a, b) in enumerate(CHUNKS):
-        g.wait_ge(S["h%d" % c], half)
-        ap = T.sw[:, e * ND + a:e * ND + b]
+    at_helper, _ = landing(len(engs))
+    to_core = {"p": cores[partner], "a": cores[far[0]], "b": cores[far[1]]}
+    seen = []
+    for call in HCALLS:
+        for to, c0, c1 in call:
+            for c, (end, n) in at_helper.items():
+                if c < c1 and c0 < end and c not in seen:
+                    g.wait_ge(S["h%d" % c], n)
+                    seen.append(c)
         g.remote_dma_fused([
-            RemoteDMATransfer(dst_ids=[dst_id(topo, cores[q])], dma_engine_mask=bits(engs[i::2]),
-                              remote_sem=S.sarr, src=ap, dst=ap) for i, q in enumerate(far)], local_sem=S.sleft)
-    g.wait_ge(S.sleft, 2 * half * len(CHUNKS))
+            RemoteDMATransfer(dst_ids=[dst_id(topo, to_core[to])], dma_engine_mask=bits(engs[i::len(call)]),
+                              remote_sem=S.sarr, src=piece(T, e, c0, c1), dst=piece(T, e, c0, c1))
+            for i, (to, c0, c1) in enumerate(call)], local_sem=S.sleft)
+    g.wait_ge(S.sleft, len(engs) * len(HCALLS))
 
 
 def rank_program(g, core, T, topo):
@@ -102,13 +127,14 @@ def rank_program(g, core, T, topo):
     if rank is None:
         for e in range(N):
             if rl[e][2] == core:
-                helper_program(g, core, T, topo, e, rl[e][1])
+                helper_program(g, core, T, topo, e, rl[e][0], rl[e][1])
         return
     S = T.sem
     V, SC, PE, SY = g.vector, g.scalar, g.tensor, g.sync
     partner, far, helper = rl[rank]
     engs = topo.engines(core, cores[partner])
-    half = len(engs) // 2
+    ne = len(engs)
+    to_core = {"h": helper, "p": cores[partner], "a": cores[far[0]], "b": cores[far[1]]}
     nsem = [0]
 
     def new():
@@ -132,47 +158,75 @@ def rank_program(g, core, T, topo):
 
     tw, sw = T.tw, T.sw
     c_own, c_par, c_f0, c_f1 = rank * W, partner * W, far[0] * W, far[1] * W
+    seen, e_ld = [], []
 
-    def load(c):
-        a, b = CHUNKS[c]
-        return sig(SY.dma_start(sw[:, rank * ND + a:rank * ND + b], T.sums[:, a:b]), 16)
+    def load(loads):
+        for c0, c1 in loads:
+            e = sig(SY.dma_start(piece(T, rank, c0, c1), T.sums[:, CHUNKS[c0][0]:CHUNKS[c1 - 1][1]]), 16)
+            e_ld.extend([e] * (c1 - c0))
+
+    def send(call):
+        trs = []
+        for i, (to, c0, c1) in enumerate(call):
+            for c in range(c0, c1):
+                if e_ld[c] not in seen:
+                    wait(g, e_ld[c])
+                    seen.append(e_ld[c])
+            ap = piece(T, rank, c0, c1)
+            trs.append(RemoteDMATransfer(
+                dst_ids=[dst_id(topo, to_core[to])], dma_engine_mask=bits(engs[i::len(call)]),
+                remote_sem=S["h%d" % c0] if to == "h" else S.sarr, src=ap, dst=ap))
+        g.remote_dma_fused(trs, local_sem=S.sleft)
 
     e_ci = sig(SY.dma_start(T.ci[:], T.child[:]), 16)
-    e_ld = [load(c) for c in range(FRONT)]
-    e_q = group([SY.dma_start(T.di[:], T.day[:]), SY.dma_start(T.vi[:], T.ver[:])], 16)
+    load(LOADS[0])
 
-    e_fz = sig(V.memset(tw[:, c_f0:c_f0 + 1024], 0.0))
+    e_fz = [sig(V.memset(tw[:, c_f0:c_f0 + ZB], 0.0)), sig(V.memset(tw[:, c_f0 + ZB:c_f0 + 1024], 0.0))]
     s_own = new()
-    V.memset(tw[:, c_own:c_own + 2560], 0.0).then_inc(s_own, 1)
+    V.memset(tw[:, c_own:c_own + V1], 0.0).then_inc(s_own, 1)
     wait(V, e_ci)
     e_hi = sig(V.tensor_copy(T.hi[:], T.ci[:]))
     wait(V, e_hi)
     e_lo = sig(V.tensor_tensor(T.lo[:], T.ci[:], T.hi[:], A.subtract))
-    V.memset(tw[:, c_own + 2560:c_own + W], 0.0).then_inc(s_own, 1)
+    V.memset(tw[:, c_own + V1:c_own + W], 0.0).then_inc(s_own, 1)
     e_own = (s_own, 2)
     e_fpar = sig(V.memset(tw[:, c_par:c_par + W], 0.0))
-    e_ff0 = sig(V.memset(tw[:, c_f0 + 3248:c_f0 + W], 0.0))
+    c_l = c_f0 + 1024 + ZB
+    c_s = c_l + LZ
+    e_ff0 = sig(V.memset(tw[:, c_s + SF:c_f0 + W], 0.0))
+    wait(SY, *e_fz)
+    e_lz = group([SY.dma_start(tw[:, c_l + a:c_l + min(LZ, a + 1024)], tw[:, c_f0:c_f0 + min(1024, LZ - a)])
+                  for a in range(0, LZ, 1024)], 16)
 
-    wait(SC, e_fz)
-    z = tw[:, c_f0:c_f0 + 1024]
-    e_ff1 = group([SC.activation(tw[:, c_f1 + a:c_f1 + a + 1024], z, COPY) for a in range(0, W, 1024)])
-    e_fs = group([SC.activation(tw[:, c_f0 + 2048:c_f0 + 3072], z, COPY),
-                  SC.activation(tw[:, c_f0 + 3072:c_f0 + 3248], tw[:, c_f0:c_f0 + 176], COPY)])
+    def zeros(c0, n, step):
+        return [SC.activation(tw[:, c0 + a:c0 + min(n, a + step)], tw[:, c_f0:c_f0 + min(step, n - a)], COPY)
+                for a in range(0, n, step)]
+
+    wait(SC, e_fz[0])
+    ff1 = zeros(c_f1, ZB, ZB)
+    wait(SC, e_fz[1])
+    e_ff1 = group(ff1 + zeros(c_f1 + ZB, W - ZB, 1024))
+    e_fs = group(zeros(c_s, SF, 1024))
     filled = {partner: [e_fpar], far[1]: [e_ff1],
-              far[0]: [e_ff1, e_fs, e_ff0, (S.zarr, 2 * half), (S.zleft, 2 * half)]}
+              far[0]: [e_ff1, e_fs, e_ff0, e_lz, (S.zarr, ne), (S.zleft, ne)]}
 
-    i_val = g.iota(T.val[:], [[1, 144]], 0, -1, allow_small_or_imprecise_dtypes=True)
-    wait(g, e_fz)
-    c_z = rl[partner][1][0] * W
+    wait(g, e_fz[0])
+    c_z = rl[partner][1][0] * W + 1024
     rid, pid, _ = topo.addr(cores[partner])
-    g.remote_dma(tw[:, c_z + 1024:c_z + 2048], z, S.zarr, S.zleft, pid, rid, bits(engs))
-    e_val = group([i_val, g.iota(T.pi[:, 0:1], [[1, 1]], 127, -1)])
+    g.remote_dma(tw[:, c_z:c_z + ZB], tw[:, c_f0:c_f0 + ZB], S.zarr, S.zleft, pid, rid, bits(engs))
     others = [partner] + far
     wait(g, e_lo)
     g.remote_dma_fused([
         RemoteDMATransfer(dst_ids=[dst_id(topo, cores[q]) for q in others], dma_engine_mask=bits(engs[i::2]),
                           remote_sem=S["tab%d" % rank], srcs=[src[:]], dsts=[T.td[2 * rank + i] for q in others])
         for i, src in enumerate((T.hi, T.lo))], local_sem=S.tleft)
+    for call in CALLS[:GAP]:
+        send(call)
+    wait(g, sig(g.iota(T.B[:], [[0, 144]], 0, 0, allow_small_or_imprecise_dtypes=True)))
+    e_t = sig(g.affine_select(T.two[:], T.B[:, 0:8], [[16, 8]], A.is_gt, 2.0, 0, -1))
+    e_ib = sig(g.affine_select(T.Ib[:], T.B[:, 0:128], [[-1, 128]], A.not_equal, 1.0, 0, 1))
+    wait(g, e_t, e_ib)
+    e_b = sig(g.affine_select(T.B[:, 15:143:16], T.two[:], [[16, 8]], A.is_ge, 0.0, 15, -1))
 
     tdma = new()
     ntd = 0
@@ -180,158 +234,203 @@ def rank_program(g, core, T, topo):
     for i, src in enumerate((T.hi, T.lo)):
         SY.dma_start(tw[i::16, c_own:c_own + W], src[:]).then_inc(tdma, 16)
         ntd += 16
+    e_q = group([SY.dma_start(T.di[:], T.day[:]), SY.dma_start(T.vi[:], T.ver[:])], 16)
     for r in (far[1], partner, far[0]):
         qs = (SY, SC) if r == far[0] else (SY, SY)
         for i, q in enumerate(qs):
             if i == 0 or q is not qs[0]:
                 wait(q, *filled[r])
-                q.wait_ge(S["tab%d" % r], 2 * half)
+                q.wait_ge(S["tab%d" % r], ne)
             q.dma_start(tw[i::16, r * W:(r + 1) * W], T.td[2 * r + i]).then_inc(tdma, 16)
             ntd += 16
     e_tw = (tdma, ntd)
     s_iss = new()
     SY.sem_inc(s_iss, 1)
-    e_ld += [load(c) for c in range(FRONT, len(CHUNKS))]
+    load(LOADS[1])
 
-    seen = []
-    for n, call in enumerate(CALLS):
-        if n == GAP:
-            g.wait_ge(s_iss, 1)
-        trs = []
-        for i, (to, c) in enumerate(call):
-            if c not in seen:
-                wait(g, e_ld[c])
-                seen.append(c)
-            ap = sw[:, rank * ND + CHUNKS[c][0]:rank * ND + CHUNKS[c][1]]
-            trs.append(RemoteDMATransfer(
-                dst_ids=[dst_id(topo, helper if to == "h" else cores[partner])], dma_engine_mask=bits(engs[i::2]),
-                remote_sem=S["h%d" % c] if to == "h" else S.sarr, src=ap, dst=ap))
-        g.remote_dma_fused(trs, local_sem=S.sleft)
-    g.wait_ge(S.tleft, 2 * half)
-    g.wait_ge(S.sleft, 2 * half * len(CALLS))
-    e_sums = [(S.sarr, 3 * half * len(CHUNKS))] + e_ld
+    g.wait_ge(s_iss, 1)
+    for call in CALLS[GAP:]:
+        send(call)
+    g.wait_ge(S.tleft, ne)
+    g.wait_ge(S.sleft, ne * len(CALLS))
+    e_sums = [(S.sarr, landing(ne)[1])] + seen
 
     def col(t, a=0, b=K):
         return slice(t * K + a, t * K + b)
 
+    def steps(t0, t1):
+        return slice(t0 * K, t1 * K)
+
+    def bit(t):
+        return V.tensor_scalar(T.bi[:, col(t)], T.di[:], last - t, 1, A.logical_shift_right, A.bitwise_and)
+
     last = D - 1
-    wait(V, e_q, e_val)
-    e_bi = group([V.tensor_scalar(T.pa[:, 0:1], T.pi[:, 0:1], 15, None, A.bitwise_and),
-                  V.tensor_scalar(T.v2[:], T.vi[:], 2.0, None, A.mult),
-                  V.tensor_scalar(T.bi[:, col(0)], T.di[:], last, 1, A.logical_shift_right, A.bitwise_and)])
-    e_b2 = group([V.tensor_scalar(T.bi[:, col(t)], T.di[:], last - t, 1, A.logical_shift_right, A.bitwise_and)
-                  for t in range(1, D)])
+    wait(V, e_q)
+    e_bi = group([bit(0), V.tensor_scalar(T.v2[:], T.vi[:], 2.0, None, A.mult)])
+    e_b1 = group([bit(t) for t in range(1, PRE)])
     wait(V, e_bi)
-    e_c1 = group([V.tensor_copy(T.pf[:, 0:1], T.pa[:, 0:1]),
-                  V.tensor_tensor(T.i0f[:], T.v2[:], T.bi[:, col(0)], A.add)])
-    wait(V, e_b2)
-    c2 = [V.tensor_copy(T.badd[:, K:last * K], T.bi[:, K:last * K]),
-          V.tensor_scalar(T.Ib[:], T.val[:, 0:128], 0.0, None, A.is_equal)]
+    e_c1 = sig(V.tensor_tensor(T.i0f[:], T.v2[:], T.bi[:, col(0)], A.add))
+    wait(V, e_b1)
+    e_w1 = sig(V.tensor_copy(T.badd[:, steps(0, PRE)], T.bi[:, steps(0, PRE)]))
     wait(V, e_c1)
     e_i0 = sig(V.tensor_copy(T.idx[:, col(0)], T.i0f[:]))
-    c2 += [V.tensor_scalar(T.B[:], T.val[:], T.pf[:, 0:1], 2.0, A.is_equal, A.mult),
-           V.tensor_scalar(T.badd[:, col(last)], T.bi[:, col(last)], -16384.0, 16384.0, A.mult, A.add),
-           V.tensor_scalar(T.If[:], T.val[:, 0:128], 0.0, None, A.is_equal)]
-    wait(PE, group(c2))
-    e_c3 = group([V.tensor_scalar(T.cmax[:, 0:last * K], T.bi[:, 0:last * K], -16385.0, 16385.0, A.mult, A.add),
-                  V.memset(sw[:, N * ND:N * ND + 8], 0.0)])
+    wait(PE, e_w1, e_b)
 
-    e_u, e_off = {}, {}
-
-    def off_a(t, src):
-        e_u[t] = sig(V.tensor_tensor(T.u[:, col(t)], src, T.cmax[:, col(t)], A.max))
-
-    def off_b(t):
-        wait(V, e_u[t])
-        e_off[t] = sig(V.tensor_scalar(T.off[:, col(t)], T.u[:, col(t)], -1.0, 0.5, A.add, A.mult))
-
-    st = {"v": None, "first": True, "n": 0}
+    e_off, ev, waited = {}, {}, []
+    st = {"v": None, "nv": 0, "ns": 0}
     pend = []
 
-    def totals_v(t):
-        first = st["v"] is None
-        if first:
-            wait(V, *e_sums)
+    def need(q, *names):
+        for n in names:
+            if (q is V, n) not in waited:
+                wait(q, ev[n])
+                waited.append((q is V, n))
+
+    def small(job):
+        early, late = steps(0, TWO), steps(TWO, last)
+        if job[0] == "b":
+            ev[job] = sig(bit(int(job[1])))
+        elif job == "w":
+            need(V, *["b%d" % x for x in range(PRE, D)])
+            ev["w"] = ev["badd", PRE - 1] = sig(V.tensor_copy(T.badd[:, steps(PRE, D)], T.bi[:, steps(PRE, D)]))
+        elif job == "w7":
+            need(SC, "w")
+            ev["badd", last - 1] = sig(SC.activation(T.badd[:, col(last)], T.badd[:, col(last)], IDENT,
+                                                     bias=16384.0, scale=-16384.0))
+        elif job in ("c0", "c1"):
+            wait(SC, e_w1)
+            need(SC, "w")
+            c, big = (early, 8192.0) if job == "c0" else (late, 16385.0)
+            ev[job] = sig(SC.activation(T.cmax[:, c], T.badd[:, c], IDENT, bias=big, scale=-big))
+        elif job == "zero":
+            wait(SC, e_b)
+            ev[job] = sig(SC.activation(sw[:, N * ND:N * ND + 8], T.two[:], COPY, scale=0.0))
+        elif job == "If":
+            wait(SC, e_b)
+            ev[job] = sig(SC.activation(T.If[:], T.Ib[:], COPY))
+        elif job == "n":
+            ev[job] = sig(V.tensor_scalar(T.nf[:, early], T.idx[:, early], -1.0, 0.5, A.add, A.mult))
+        elif job == "m":
+            need(V, "c0", "n")
+            ev[job] = sig(V.tensor_tensor(T.u[:, early], T.nf[:, early], T.cmax[:, early], A.max))
+        elif job == "l":
+            need(V, "m")
+            e = sig(V.tensor_copy(T.off[:, early], T.u[:, early]))
+            e_off.update({t: e for t in range(TWO)})
+        elif job == "a57":
+            c = steps(TWO + 1, last)
+            ev["a"].append(sig(V.tensor_tensor(T.u[:, c], T.ps4[:, 0:(last - TWO - 1) * K], T.cmax[:, c], A.max)))
+        elif job == "o":
+            wait(V, *ev["a"])
+            e = sig(V.tensor_scalar(T.off[:, late], T.u[:, late], -1.0, 0.5, A.add, A.mult))
+            e_off.update({t: e for t in range(TWO, last)})
+
+    def totals_v(parts):
+        t = st["nv"]
+        st["nv"] += 1
+        if t == 0:
+            wait(V, ev["zero"], *e_sums)
         wait(V, e_off[t])
         evs = []
-        for i, (a, b) in enumerate(VPARTS):
+        for a, b in parts:
             src = sw[:].indirect(T.off[:, col(t, a, b)])
             acc = T.acc[:, 16 * a:16 * b]
-            if first:
-                evs.append(sig(V.tensor_copy(acc, src)))
+            if t == 0:
+                evs.append((a, b, sig(V.tensor_copy(acc, src))))
             else:
-                wait(V, st["v"][i])
-                evs.append(sig(V.tensor_tensor(acc, src, acc, A.add)))
+                wait(V, *[e for x, y, e in st["v"] if x < b and a < y])
+                evs.append((a, b, sig(V.tensor_tensor(acc, src, acc, A.add))))
         st["v"] = evs
 
-    def totals_s(t):
-        if st["first"]:
-            wait(SC, *e_sums)
-            st["first"] = False
-        wait(SC, e_off[t])
-        pend.append((t, sig(SC.activation(T.gs[:, t * QS:(t + 1) * QS], sw[:].indirect(T.off[:, col(t, KV, K)]),
-                                          COPY))))
+    def gs(t, a, b):
+        return T.gs[:, t * QS + 16 * (a - KV):t * QS + 16 * (b - KV)]
 
-    def totals_pe():
-        mm = None
-        while pend:
-            t, ev = pend.pop(0)
-            wait(PE, ev)
-            mm = PE.matmul(T.pacc[:, 0:QS], T.If[:], T.gs[:, t * QS:(t + 1) * QS], st["n"] == 0, st["n"] == D - 1)
-            st["n"] += 1
-        return mm
-
-    wait(V, e_i0, e_c3, e_tw)
-    wait(SC, e_i0, e_tw)
-    done_v, done_s = [], []
-    e_pe = None
-    for t in range(last):
-        ps = T["ps%d" % t]
-        res = T.i0f[:]
-        if t > 0:
-            res = T["ps%d" % (t - 1)][:, 0:K]
-            wait(V, e_pe)
-            e_idx = sig(V.tensor_copy(T.idx[:, col(t)], res))
-            off_a(t, res)
-            wait(V, e_idx)
-            wait(SC, e_idx)
-        g0 = t * Q
-        e_g = group([V.tensor_copy(T.G[:, g0:g0 + 16 * KG], tw[:].indirect(T.idx[:, col(t, 0, KG)])),
-                     SC.activation(T.G[:, g0 + 16 * KG:g0 + Q], tw[:].indirect(T.idx[:, col(t, KG, K)]), COPY)])
-        PE.matmul(ps[:, 0:K], T.Ib[:], T.badd[:, col(t + 1)], True, False)
-        if PE_EARLY:
-            totals_pe()
-        wait(PE, e_g)
-        for s in range(16):
-            mm = PE.matmul(ps[:, 0:K], T.B[:, 15 - s:143 - s], T.G[:, g0 + s:g0 + Q:16], False, s == 15)
-        e_pe = sig(mm)
+    def totals_s():
+        t = st["ns"]
+        st["ns"] += 1
         if t == 0:
-            off_a(0, res)
-        else:
-            off_b(t)
-        if t == 1:
-            off_b(0)
-        for x in EARLY_V.get(t, []):
-            totals_v(x)
-            done_v.append(x)
-        for x in EARLY_S.get(t, []):
-            totals_s(x)
-            done_s.append(x)
+            wait(SC, ev["zero"], *e_sums)
+            wait(PE, ev["If"])
+        wait(SC, e_off[t])
+        pend.append((t, [sig(SC.activation(gs(t, a, b), sw[:].indirect(T.off[:, col(t, a, b)]), COPY))
+                         for a, b in ([(KV, K)] if t < last else SHALVES)]))
 
-    rest = [t for t in range(last) if t not in done_v]
-    totals_v(rest[0])
-    wait(V, e_pe)
-    e_off[last] = sig(V.tensor_scalar(T.off[:, col(last)], T["ps%d" % (last - 1)][:, 0:K], 0.5, float(N * ND),
-                                      A.mult, A.min))
-    for t in rest[1:] + [last]:
-        totals_v(t)
-    for t in range(D):
-        if t not in done_s:
-            totals_s(t)
-    e_acc = sig(totals_pe())
+    def totals_pe(n):
+        mms = []
+        for _ in range(n):
+            t, evs = pend.pop(0)
+            mms = []
+            for i, (a, b) in enumerate(SHALVES):
+                if i < len(evs):
+                    wait(PE, evs[i])
+                mms.append(PE.matmul(T["pacc%d" % i][:, 0:16 * (b - a)], T.If[:], gs(t, a, b), t == 0, t == last))
+        return mms
 
-    wait(SY, *st["v"])
+    def jobs(names):
+        for job in names.split():
+            if job in ("T", "H"):
+                totals_v([(0, KV)] if job == "T" else VHALVES)
+            elif job == "S":
+                totals_s()
+            else:
+                small(job)
+
+    wait(V, e_tw)
+    wait(SC, e_tw)
+    made, w = [], 0
+    ev["a"] = []
+    for t in range(last):
+        src, made = made, []
+        for h, (a, b) in enumerate([(0, H), (H, K)] if t < TWO else [(0, K)]):
+            e_idx = [e_i0] if t == 0 else []
+            while src and src[0][0] < b:
+                x, y, reg, e = src.pop(0)
+                wait(V, e)
+                e_idx.append(sig(V.tensor_copy(T.idx[:, col(t, x, y)], reg)))
+                if t == TWO:
+                    need(V, "c1")
+                    ev["a"].append(sig(V.tensor_tensor(T.u[:, col(t, x, y)], reg, T.cmax[:, col(t, x, y)], A.max)))
+                    if x == 0:
+                        small("l")
+            jobs(SLOT[w])
+            g0, m = t * Q, a + KG[w]
+            wait(V, *e_idx)
+            wait(SC, *e_idx)
+            e_g = group([
+                V.tensor_copy(T.G[:, g0 + 16 * a:g0 + 16 * m], tw[:].indirect(T.idx[:, col(t, a, m)])),
+                SC.activation(T.G[:, g0 + 16 * m:g0 + 16 * b], tw[:].indirect(T.idx[:, col(t, m, b)]), COPY)])
+            if h == 0 and ("badd", t) in ev:
+                wait(PE, ev["badd", t])
+            totals_pe(PJ[w])
+            if t < TWO:
+                ps = T["ps%d" % (2 * (t % 2) + h)][:, 0:H]
+            elif t < last - 1:
+                ps = T.ps4[:, col(t - TWO)]
+                if t > TWO:
+                    wait(PE, *e_idx)
+            else:
+                ps = T.ps5[:, 0:K]
+            PE.matmul(ps, T.Ib[:], T.badd[:, col(t + 1, a, b)], True, False)
+            wait(PE, e_g)
+            for s in range(16):
+                mm = PE.matmul(ps, T.B[:, 15 - s:143 - s], T.G[:, g0 + 16 * a + s:g0 + 16 * b:16], False, s == 15)
+            made.append((a, b, ps, sig(mm)))
+            jobs(JOBS[w])
+            w += 1
+
+    wait(V, made[0][3])
+    e_off[last] = sig(V.tensor_scalar(T.off[:, col(last)], ps, 0.5, float(N * ND), A.mult, A.min))
+    while st["nv"] < D:
+        totals_v(VHALVES)
+    while st["ns"] < D:
+        totals_s()
+    e_acc = [sig(mm) for mm in totals_pe(len(pend))]
+
+    wait(SY, *[e for a, b, e in st["v"]])
     wait(SY, sig(SY.dma_start(T.y[:, 0:QV], T.acc[:]), 16))
-    wait(SC, e_acc)
-    wait(SC, sig(SC.activation(T.out2[:], T.pacc[:, 0:QS], COPY)))
+    outs = []
+    for i, (a, b) in enumerate(SHALVES):
+        wait(SC, e_acc[i])
+        outs.append(SC.activation(T.out2[:, 16 * (a - KV):16 * (b - KV)], T["pacc%d" % i][:, 0:16 * (b - a)], COPY))
+    wait(SC, group(outs))
     wait(SC, sig(SC.dma_start(T.y[:, QV:Q], T.out2[:]), 16))

from concourse.bass import DstId, RemoteDMATransfer
from concourse.mybir import AluOpType, ActivationFunctionType

N, ND, D, Q = 4, 2048, 8, 512
K = Q // 16
H = K // 2
KV = 16
QV, QS = 16 * KV, Q - 16 * KV
VHALVES = [(0, KV // 4 * 2), (KV // 4 * 2, KV)]
SHALVES = [(KV, KV + 10), (KV + 10, K)]
CHUNKS = [(0, 512), (512, 1024), (1024, 1536), (1536, 2048)]
CALLS = [(("h", 0, 1),), (("h", 1, 2), ("p", 1, 2)), (("h", 2, 3), ("p", 2, 3)), (("a", 3, 4), ("p", 3, 4)), (("b", 3, 4),)]
HCALLS = [(("p", 0, 1), ("a", 0, 1)), (("b", 0, 1),), (("a", 1, 2), ("b", 1, 2)), (("a", 2, 3), ("b", 2, 3))]
GAP = 1
LOADS = [[(0, 2)], [(2, 3), (3, 4)]]
ZB = 256
LZ = 1792
V1 = 2048
SF = 640
TWO = 5
PRE = 4
KG = [8, 8, 8, 8, 8, 8, 8, 8, 8, 8, 16, 16]
SLOT = ["", "", "", "", "", "", "", "", "", "", "", "a57"]
JOBS = ["b4 b5 If", "b6 b7 zero", "w", "c0", "c1", "w7", "", "", "", "n m", "H H S S S", "o H H"]
PJ = [0, 0, 0, 0, 0, 0, 0, 0, 0, 0, 0, 3]
W = 2 * ND

SCRATCH = {
    "ci": ("sbuf", [128, 256], "int32"),
    "hi": ("sbuf", [128, 256], "bfloat16"),
    "lo": ("sbuf", [128, 256], "bfloat16"),
    "td": ("dram", [2 * N, 128, 256], "bfloat16"),
    "tw": ("sbuf", [128, N * W], "bfloat16"),
    "sw": ("sbuf", [128, N * ND + 8], "float32"),
    "vi": ("sbuf", [128, K], "int32"),
    "di": ("sbuf", [128, K], "int32"),
    "bi": ("sbuf", [128, D * K], "int32"),
    "badd": ("sbuf", [128, D * K], "bfloat16"),
    "cmax": ("sbuf", [128, D * K], "float32"),
    "v2": ("sbuf", [128, K], "float32"),
    "i0f": ("sbuf", [128, K], "float32"),
    "idx": ("sbuf", [128, D * K], "uint16"),
    "off": ("sbuf", [128, D * K], "uint16"),
    "nf": ("sbuf", [128, D * K], "float32"),
    "u": ("sbuf", [128, D * K], "float32"),
    "G": ("sbuf", [128, (D - 1) * Q], "bfloat16"),
    "two": ("sbuf", [128, 8], "bfloat16"),
    "B": ("sbuf", [128, 144], "bfloat16"),
    "Ib": ("sbuf", [128, 128], "bfloat16"),
    "If": ("sbuf", [128, 128], "float32"),
    "acc": ("sbuf", [128, QV], "float32"),
    "gs": ("sbuf", [128, D * QS], "float32"),
    "out2": ("sbuf", [128, QS], "float32"),
    "pacc0": ("psum", [128, 512], "float32"),
    "pacc1": ("psum", [128, 512], "float32"),
}
for _t in range(6):
    SCRATCH["ps%d" % _t] = ("psum", [128, 512], "float32")

SEMAPHORES = (["tab%d" % r for r in range(N)] + ["h%d" % c for c in range(len(CHUNKS))]
              + ["sarr", "tleft", "sleft", "zarr", "zleft"] + ["s%d" % i for i in range(130)])

A = AluOpType
COPY = ActivationFunctionType.Copy
IDENT = ActivationFunctionType.Identity


def bits(engs):
    m = 0
    for e in engs:
        m |= 1 << e
    return m


def dst_id(topo, c):
    rid, pid, _ = topo.addr(c)
    return DstId(rid=rid, pnc=pid)


def roles(T, topo):
    cores = list(T.cores)
    free = [c for c in topo.cores_of(cores[0]) if c not in cores]
    out = []
    for r, c in enumerate(cores):
        near = [q for q in range(N) if topo.die(cores[q]) == topo.die(c)]
        far = [q for q in range(N) if q not in near]
        helpers = [h for h in free if topo.die(h) != topo.die(c)]
        i = near.index(r)
        out.append(([q for q in near if q != r][0], far[i:] + far[:i], helpers[i]))
    return out


def piece(T, e, c0, c1):
    return T.sw[:, e * ND + CHUNKS[c0][0]:e * ND + CHUNKS[c1 - 1][1]]


def landing(n_eng):
    at_helper = {c0: (c1, n_eng // len(call)) for call in CALLS for to, c0, c1 in call if to == "h"}
    at_rank = sum(n_eng // len(call) for call in CALLS for to, c0, c1 in call if to != "h")
    return at_helper, at_rank + n_eng * len(HCALLS)


def helper_program(g, core, T, topo, e, partner, far):
    cores = list(T.cores)
    S = T.sem
    engs = topo.engines(core, cores[far[0]])
    at_helper, _ = landing(len(engs))
    to_core = {"p": cores[partner], "a": cores[far[0]], "b": cores[far[1]]}
    seen = []
    for call in HCALLS:
        for to, c0, c1 in call:
            for c, (end, n) in at_helper.items():
                if c < c1 and c0 < end and c not in seen:
                    g.wait_ge(S["h%d" % c], n)
                    seen.append(c)
        g.remote_dma_fused([
            RemoteDMATransfer(dst_ids=[dst_id(topo, to_core[to])], dma_engine_mask=bits(engs[i::len(call)]),
                              remote_sem=S.sarr, src=piece(T, e, c0, c1), dst=piece(T, e, c0, c1))
            for i, (to, c0, c1) in enumerate(call)], local_sem=S.sleft)
    g.wait_ge(S.sleft, len(engs) * len(HCALLS))


def rank_program(g, core, T, topo):
    rank = T.rank_of(core)
    cores = list(T.cores)
    rl = roles(T, topo)
    if rank is None:
        for e in range(N):
            if rl[e][2] == core:
                helper_program(g, core, T, topo, e, rl[e][0], rl[e][1])
        return
    S = T.sem
    V, SC, PE, SY = g.vector, g.scalar, g.tensor, g.sync
    partner, far, helper = rl[rank]
    engs = topo.engines(core, cores[partner])
    ne = len(engs)
    to_core = {"h": helper, "p": cores[partner], "a": cores[far[0]], "b": cores[far[1]]}
    nsem = [0]

    def new():
        nsem[0] += 1
        return S["s%d" % (nsem[0] - 1)]

    def sig(ins, n=1):
        s = new()
        ins.then_inc(s, n)
        return (s, n)

    def group(inss, n=1):
        s = new()
        for i in inss:
            i.then_inc(s, n)
        return (s, n * len(inss))

    def wait(q, *evs):
        for s, n in evs:
            q.wait_ge(s, n)

    tw, sw = T.tw, T.sw
    c_own, c_par, c_f0, c_f1 = rank * W, partner * W, far[0] * W, far[1] * W
    seen, e_ld = [], []

    def load(loads):
        for c0, c1 in loads:
            e = sig(SY.dma_start(piece(T, rank, c0, c1), T.sums[:, CHUNKS[c0][0]:CHUNKS[c1 - 1][1]]), 16)
            e_ld.extend([e] * (c1 - c0))

    def send(call):
        trs = []
        for i, (to, c0, c1) in enumerate(call):
            for c in range(c0, c1):
                if e_ld[c] not in seen:
                    wait(g, e_ld[c])
                    seen.append(e_ld[c])
            ap = piece(T, rank, c0, c1)
            trs.append(RemoteDMATransfer(
                dst_ids=[dst_id(topo, to_core[to])], dma_engine_mask=bits(engs[i::len(call)]),
                remote_sem=S["h%d" % c0] if to == "h" else S.sarr, src=ap, dst=ap))
        g.remote_dma_fused(trs, local_sem=S.sleft)

    e_ci = sig(SY.dma_start(T.ci[:], T.child[:]), 16)
    load(LOADS[0])

    e_fz = [sig(V.memset(tw[:, c_f0:c_f0 + ZB], 0.0)), sig(V.memset(tw[:, c_f0 + ZB:c_f0 + 1024], 0.0))]
    s_own = new()
    V.memset(tw[:, c_own:c_own + V1], 0.0).then_inc(s_own, 1)
    wait(V, e_ci)
    e_hi = sig(V.tensor_copy(T.hi[:], T.ci[:]))
    wait(V, e_hi)
    e_lo = sig(V.tensor_tensor(T.lo[:], T.ci[:], T.hi[:], A.subtract))
    V.memset(tw[:, c_own + V1:c_own + W], 0.0).then_inc(s_own, 1)
    e_own = (s_own, 2)
    e_fpar = sig(V.memset(tw[:, c_par:c_par + W], 0.0))
    c_l = c_f0 + 1024 + ZB
    c_s = c_l + LZ
    e_ff0 = sig(V.memset(tw[:, c_s + SF:c_f0 + W], 0.0))
    wait(SY, *e_fz)
    e_lz = group([SY.dma_start(tw[:, c_l + a:c_l + min(LZ, a + 1024)], tw[:, c_f0:c_f0 + min(1024, LZ - a)])
                  for a in range(0, LZ, 1024)], 16)

    def zeros(c0, n, step):
        return [SC.activation(tw[:, c0 + a:c0 + min(n, a + step)], tw[:, c_f0:c_f0 + min(step, n - a)], COPY)
                for a in range(0, n, step)]

    wait(SC, e_fz[0])
    ff1 = zeros(c_f1, ZB, ZB)
    wait(SC, e_fz[1])
    e_ff1 = group(ff1 + zeros(c_f1 + ZB, W - ZB, 1024))
    e_fs = group(zeros(c_s, SF, 1024))
    filled = {partner: [e_fpar], far[1]: [e_ff1],
              far[0]: [e_ff1, e_fs, e_ff0, e_lz, (S.zarr, ne), (S.zleft, ne)]}

    wait(g, e_fz[0])
    c_z = rl[partner][1][0] * W + 1024
    rid, pid, _ = topo.addr(cores[partner])
    g.remote_dma(tw[:, c_z:c_z + ZB], tw[:, c_f0:c_f0 + ZB], S.zarr, S.zleft, pid, rid, bits(engs))
    others = [partner] + far
    wait(g, e_lo)
    g.remote_dma_fused([
        RemoteDMATransfer(dst_ids=[dst_id(topo, cores[q]) for q in others], dma_engine_mask=bits(engs[i::2]),
                          remote_sem=S["tab%d" % rank], srcs=[src[:]], dsts=[T.td[2 * rank + i] for q in others])
        for i, src in enumerate((T.hi, T.lo))], local_sem=S.tleft)
    for call in CALLS[:GAP]:
        send(call)
    wait(g, sig(g.iota(T.B[:], [[0, 144]], 0, 0, allow_small_or_imprecise_dtypes=True)))
    e_t = sig(g.affine_select(T.two[:], T.B[:, 0:8], [[16, 8]], A.is_gt, 2.0, 0, -1))
    e_ib = sig(g.affine_select(T.Ib[:], T.B[:, 0:128], [[-1, 128]], A.not_equal, 1.0, 0, 1))
    wait(g, e_t, e_ib)
    e_b = sig(g.affine_select(T.B[:, 15:143:16], T.two[:], [[16, 8]], A.is_ge, 0.0, 15, -1))

    tdma = new()
    ntd = 0
    wait(SY, e_lo, e_own)
    for i, src in enumerate((T.hi, T.lo)):
        SY.dma_start(tw[i::16, c_own:c_own + W], src[:]).then_inc(tdma, 16)
        ntd += 16
    e_q = group([SY.dma_start(T.di[:], T.day[:]), SY.dma_start(T.vi[:], T.ver[:])], 16)
    for r in (far[1], partner, far[0]):
        qs = (SY, SC) if r == far[0] else (SY, SY)
        for i, q in enumerate(qs):
            if i == 0 or q is not qs[0]:
                wait(q, *filled[r])
                q.wait_ge(S["tab%d" % r], ne)
            q.dma_start(tw[i::16, r * W:(r + 1) * W], T.td[2 * r + i]).then_inc(tdma, 16)
            ntd += 16
    e_tw = (tdma, ntd)
    s_iss = new()
    SY.sem_inc(s_iss, 1)
    load(LOADS[1])

    g.wait_ge(s_iss, 1)
    for call in CALLS[GAP:]:
        send(call)
    g.wait_ge(S.tleft, ne)
    g.wait_ge(S.sleft, ne * len(CALLS))
    e_sums = [(S.sarr, landing(ne)[1])] + seen

    def col(t, a=0, b=K):
        return slice(t * K + a, t * K + b)

    def steps(t0, t1):
        return slice(t0 * K, t1 * K)

    def bit(t):
        return V.tensor_scalar(T.bi[:, col(t)], T.di[:], last - t, 1, A.logical_shift_right, A.bitwise_and)

    last = D - 1
    wait(V, e_q)
    e_bi = group([bit(0), V.tensor_scalar(T.v2[:], T.vi[:], 2.0, None, A.mult)])
    e_b1 = group([bit(t) for t in range(1, PRE)])
    wait(V, e_bi)
    e_c1 = sig(V.tensor_tensor(T.i0f[:], T.v2[:], T.bi[:, col(0)], A.add))
    wait(V, e_b1)
    e_w1 = sig(V.tensor_copy(T.badd[:, steps(0, PRE)], T.bi[:, steps(0, PRE)]))
    wait(V, e_c1)
    e_i0 = sig(V.tensor_copy(T.idx[:, col(0)], T.i0f[:]))
    wait(PE, e_w1, e_b)

    e_off, ev, waited = {}, {}, []
    st = {"v": None, "nv": 0, "ns": 0}
    pend = []

    def need(q, *names):
        for n in names:
            if (q is V, n) not in waited:
                wait(q, ev[n])
                waited.append((q is V, n))

    def small(job):
        early, late = steps(0, TWO), steps(TWO, last)
        if job[0] == "b":
            ev[job] = sig(bit(int(job[1])))
        elif job == "w":
            need(V, *["b%d" % x for x in range(PRE, D)])
            ev["w"] = ev["badd", PRE - 1] = sig(V.tensor_copy(T.badd[:, steps(PRE, D)], T.bi[:, steps(PRE, D)]))
        elif job == "w7":
            need(SC, "w")
            ev["badd", last - 1] = sig(SC.activation(T.badd[:, col(last)], T.badd[:, col(last)], IDENT,
                                                     bias=16384.0, scale=-16384.0))
        elif job in ("c0", "c1"):
            wait(SC, e_w1)
            need(SC, "w")
            c, big = (early, 8192.0) if job == "c0" else (late, 16385.0)
            ev[job] = sig(SC.activation(T.cmax[:, c], T.badd[:, c], IDENT, bias=big, scale=-big))
        elif job == "zero":
            wait(SC, e_b)
            ev[job] = sig(SC.activation(sw[:, N * ND:N * ND + 8], T.two[:], COPY, scale=0.0))
        elif job == "If":
            wait(SC, e_b)
            ev[job] = sig(SC.activation(T.If[:], T.Ib[:], COPY))
        elif job == "n":
            ev[job] = sig(V.tensor_scalar(T.nf[:, early], T.idx[:, early], -1.0, 0.5, A.add, A.mult))
        elif job == "m":
            need(V, "c0", "n")
            ev[job] = sig(V.tensor_tensor(T.u[:, early], T.nf[:, early], T.cmax[:, early], A.max))
        elif job == "l":
            need(V, "m")
            e = sig(V.tensor_copy(T.off[:, early], T.u[:, early]))
            e_off.update({t: e for t in range(TWO)})
        elif job == "a57":
            c = steps(TWO + 1, last)
            ev["a"].append(sig(V.tensor_tensor(T.u[:, c], T.ps4[:, 0:(last - TWO - 1) * K], T.cmax[:, c], A.max)))
        elif job == "o":
            wait(V, *ev["a"])
            e = sig(V.tensor_scalar(T.off[:, late], T.u[:, late], -1.0, 0.5, A.add, A.mult))
            e_off.update({t: e for t in range(TWO, last)})

    def totals_v(parts):
        t = st["nv"]
        st["nv"] += 1
        if t == 0:
            wait(V, ev["zero"], *e_sums)
        wait(V, e_off[t])
        evs = []
        for a, b in parts:
            src = sw[:].indirect(T.off[:, col(t, a, b)])
            acc = T.acc[:, 16 * a:16 * b]
            if t == 0:
                evs.append((a, b, sig(V.tensor_copy(acc, src))))
            else:
                wait(V, *[e for x, y, e in st["v"] if x < b and a < y])
                evs.append((a, b, sig(V.tensor_tensor(acc, src, acc, A.add))))
        st["v"] = evs

    def gs(t, a, b):
        return T.gs[:, t * QS + 16 * (a - KV):t * QS + 16 * (b - KV)]

    def totals_s():
        t = st["ns"]
        st["ns"] += 1
        if t == 0:
            wait(SC, ev["zero"], *e_sums)
            wait(PE, ev["If"])
        wait(SC, e_off[t])
        pend.append((t, [sig(SC.activation(gs(t, a, b), sw[:].indirect(T.off[:, col(t, a, b)]), COPY))
                         for a, b in ([(KV, K)] if t < last else SHALVES)]))

    def totals_pe(n):
        mms = []
        for _ in range(n):
            t, evs = pend.pop(0)
            mms = []
            for i, (a, b) in enumerate(SHALVES):
                if i < len(evs):
                    wait(PE, evs[i])
                mms.append(PE.matmul(T["pacc%d" % i][:, 0:16 * (b - a)], T.If[:], gs(t, a, b), t == 0, t == last))
        return mms

    def jobs(names):
        for job in names.split():
            if job in ("T", "H"):
                totals_v([(0, KV)] if job == "T" else VHALVES)
            elif job == "S":
                totals_s()
            else:
                small(job)

    wait(V, e_tw)
    wait(SC, e_tw)
    made, w = [], 0
    ev["a"] = []
    for t in range(last):
        src, made = made, []
        for h, (a, b) in enumerate([(0, H), (H, K)] if t < TWO else [(0, K)]):
            e_idx = [e_i0] if t == 0 else []
            while src and src[0][0] < b:
                x, y, reg, e = src.pop(0)
                wait(V, e)
                e_idx.append(sig(V.tensor_copy(T.idx[:, col(t, x, y)], reg)))
                if t == TWO:
                    need(V, "c1")
                    ev["a"].append(sig(V.tensor_tensor(T.u[:, col(t, x, y)], reg, T.cmax[:, col(t, x, y)], A.max)))
                    if x == 0:
                        small("l")
            jobs(SLOT[w])
            g0, m = t * Q, a + KG[w]
            wait(V, *e_idx)
            wait(SC, *e_idx)
            e_g = group([
                V.tensor_copy(T.G[:, g0 + 16 * a:g0 + 16 * m], tw[:].indirect(T.idx[:, col(t, a, m)])),
                SC.activation(T.G[:, g0 + 16 * m:g0 + 16 * b], tw[:].indirect(T.idx[:, col(t, m, b)]), COPY)])
            if h == 0 and ("badd", t) in ev:
                wait(PE, ev["badd", t])
            totals_pe(PJ[w])
            if t < TWO:
                ps = T["ps%d" % (2 * (t % 2) + h)][:, 0:H]
            elif t < last - 1:
                ps = T.ps4[:, col(t - TWO)]
                if t > TWO:
                    wait(PE, *e_idx)
            else:
                ps = T.ps5[:, 0:K]
            PE.matmul(ps, T.Ib[:], T.badd[:, col(t + 1, a, b)], True, False)
            wait(PE, e_g)
            for s in range(16):
                mm = PE.matmul(ps, T.B[:, 15 - s:143 - s], T.G[:, g0 + 16 * a + s:g0 + 16 * b:16], False, s == 15)
            made.append((a, b, ps, sig(mm)))
            jobs(JOBS[w])
            w += 1

    wait(V, made[0][3])
    e_off[last] = sig(V.tensor_scalar(T.off[:, col(last)], ps, 0.5, float(N * ND), A.mult, A.min))
    while st["nv"] < D:
        totals_v(VHALVES)
    while st["ns"] < D:
        totals_s()
    e_acc = [sig(mm) for mm in totals_pe(len(pend))]

    wait(SY, *[e for a, b, e in st["v"]])
    wait(SY, sig(SY.dma_start(T.y[:, 0:QV], T.acc[:]), 16))
    outs = []
    for i, (a, b) in enumerate(SHALVES):
        wait(SC, e_acc[i])
        outs.append(SC.activation(T.out2[:, 16 * (a - KV):16 * (b - KV)], T["pacc%d" % i][:, 0:16 * (b - a)], COPY))
    wait(SC, group(outs))
    wait(SC, sig(SC.dma_start(T.y[:, QV:Q], T.out2[:]), 16))
